import numpy as np
import ml_dtypes


def mxq(x, axis, fmt="e4m3"):
    dtype, down = {"e4m3": (ml_dtypes.float8_e4m3fn, 7), "e5m2": (ml_dtypes.float8_e5m2, 14)}[fmt]
    v = np.moveaxis(np.asarray(x, np.float32).astype(ml_dtypes.bfloat16).astype(np.float64), axis, -1)
    blocks = v.reshape(v.shape[:-1] + (-1, 32))
    amax = np.abs(blocks).max(-1, keepdims=True)
    byte = np.maximum(np.where(amax > 0, np.frexp(amax)[1] - 1 + 127, 0) - down, 1)
    scale = np.exp2(byte - 127.0)
    codes = (blocks / scale).astype(np.float32).astype(dtype).astype(np.float64)
    return np.moveaxis((codes * scale).reshape(v.shape), -1, axis)


WIDE = False


def mx_kscale(k):
    if not WIDE:
        return np.ones(k)
    levels = np.array([10, -10, 5, -5, 0])
    if k % 512:
        return np.exp2(np.random.permutation(np.resize(levels, k // 32))).repeat(32)
    a = np.empty((k // 512, 16))
    for p in range(k // 512):
        a[p, :8] = np.random.permutation(np.resize(levels, 8))
        for g in range(8):
            far = levels[np.abs(levels - a[p, g]) >= 10]
            a[p, g + 8] = far[np.random.randint(len(far))]
    return np.exp2(a.ravel()).repeat(32)


def f64(x):
    return np.asarray(x).astype(np.float64)


def striped(idx):
    return np.tile(idx.reshape(-1, 16).T, (8, 1)).astype(np.uint16)


def unstriped(offs):
    return offs[:16].T.reshape(-1).astype(np.int64)


def relu(v):
    return np.maximum(v, 0.0)


K, T, E, C, H, N = 512, 4096, 8, 128, 512, 256


def by_expert(wq, xq):
    return np.concatenate([wq[e].T @ xq[:, e * C:(e + 1) * C] for e in range(E)], axis=1)


def setup_inputs():
    n = np.random.standard_normal
    s = mx_kscale(K)[:, None]
    u = mx_kscale(H)
    return {
        "xT": (n((K, T)) * s).astype(np.float32),
        "w1": (n((E, K, H)) / np.sqrt(K) / s[None] * u[None, None, :]).astype(np.float32),
        "w2": (n((E, H, N)) / np.sqrt(H) / u[None, :, None]).astype(np.float32),
        "gate": np.tile(np.random.uniform(0.2, 1.0, E * C), (N, 1)).astype(np.float32),
        "offs": striped(np.random.permutation(T)[:E * C]),
    }


def reference(xT, w1, w2, gate, offs):
    idx = unstriped(offs)
    xq = mxq(f64(xT)[:, idx], 0, "e4m3")
    h = relu(by_expert(mxq(f64(w1), 1, "e4m3"), xq))
    y = by_expert(mxq(f64(w2), 1, "e4m3"), mxq(h, 0, "e4m3"))
    out = np.zeros((N, T))
    out[:, idx] = f64(gate) * y
    return out

@@ -1,0 +1,181 @@
+from contextlib import ExitStack
+
+import concourse.mybir as mybir
+
+K, T, E, C, H, N = 512, 4096, 8, 128, 512, 256
+SLOTS = E * C
+FLOPS = 2 * SLOTS * (K * H + H * N)
+
+F32 = mybir.dt.float32
+BF16 = mybir.dt.bfloat16
+U32 = mybir.dt.uint32
+U16 = mybir.dt.uint16
+U8 = mybir.dt.uint8
+FP8X4 = mybir.dt.float8_e4m3fn_x4
+COPY = mybir.ActivationFunctionType.Copy
+RELU = mybir.ActivationFunctionType.Relu
+MULT = mybir.AluOpType.mult
+
+P = 128
+PACK = 4
+BLOCKS = N // P
+GROUPS = 2
+GE = E // GROUPS
+GS = SLOTS // GROUPS
+W1_VECTOR = 48
+W2_VECTOR = 128
+
+
+def interleave(copy, out, in_):
+    copy(
+        out=out.rearrange("p (c i t) -> p c t i", i=PACK, t=PACK),
+        in_=in_.rearrange("p t (c i) -> p c t i", i=PACK),
+    )
+
+
+def tile_routed_moe_kernel(tc, xT, w1, w2, gate, offs, out):
+    nc = tc.nc
+    with ExitStack() as ctx:
+        keep = ctx.enter_context(tc.tile_pool(name="keep", bufs=1))
+        wide = ctx.enter_context(tc.tile_pool(name="wide", bufs=6))
+        raw1 = ctx.enter_context(tc.tile_pool(name="raw1", bufs=4))
+        raw2 = ctx.enter_context(tc.tile_pool(name="raw2", bufs=4))
+        mid = ctx.enter_context(tc.tile_pool(name="mid", bufs=3))
+        codes = ctx.enter_context(tc.tile_pool(name="codes", bufs=4))
+        ps1 = ctx.enter_context(tc.psum_pool(name="ps1", bufs=4))
+        ps2 = ctx.enter_context(tc.psum_pool(name="ps2", bufs=4))
+
+        offsets = keep.tile([P, SLOTS // 16], U16, name="offsets")
+        planes = {}
+        picked = keep.tile([P, PACK, SLOTS], F32, name="picked")
+        tok = keep.tile([P, SLOTS, PACK], BF16, name="tok", align_bytes=64)
+        tok_c = keep.tile([P, SLOTS], U32, name="tok_c", align_bytes=64)
+        tok_s = keep.tile([P, SLOTS], U8, name="tok_s", align_bytes=64)
+        windows = {}
+        gates = [[keep.tile([P, GS], F32, name=f"gate{g}_{b}") for b in range(BLOCKS)] for g in range(GROUPS)]
+        sums = [keep.tile([P, BLOCKS, GS], F32, name=f"sums{g}") for g in range(GROUPS)]
+
+        for b in range(BLOCKS):
+            windows[b] = wide.tile([P, T], F32, name="wide_tile")
+        nc.vector.memset(windows[0][:], 0.0)
+        nc.gpsimd.memset(windows[1][:], 0.0)
+
+        x_planes = xT.rearrange("(p t) n -> p t n", t=PACK)
+        w1_raw, w2_raw = {}, {}
+
+        def load_plane(t):
+            planes[t] = wide.tile([P, T], F32, name="wide_tile")
+            nc.sync.dma_start(planes[t][:], x_planes[:, t, :])
+
+        def load_w1(e):
+            w1_raw[e] = raw1.tile([P, PACK, H], F32, name="w1_raw")
+            nc.sync.dma_start(w1_raw[e][:], w1[e].rearrange("(p j) h -> p j h", j=PACK))
+
+        def load_w2(e):
+            w2_raw[e] = raw2.tile([P, PACK, N], F32, name="w2_raw")
+            nc.sync.dma_start(w2_raw[e][:], w2[e].rearrange("(p j) n -> p j n", j=PACK))
+
+        def load_gate(g, b):
+            nc.sync.dma_start(gates[g][b][:], gate[b * P : (b + 1) * P, g * GS : (g + 1) * GS])
+
+        w1_codes, w2_codes = {}, {}
+
+        def prep_w1(e):
+            grouped = mid.tile([P, H * PACK], BF16, name="w1_grouped", align_bytes=64)
+            dst = grouped[:].rearrange("p (t m j) -> p m j t", t=PACK, j=PACK)
+            src = w1_raw[e][:].rearrange("p j (m t) -> p m j t", t=PACK)
+            nc.vector.tensor_copy(out=dst[:, :W1_VECTOR], in_=src[:, :W1_VECTOR])
+            nc.scalar.copy(out=dst[:, W1_VECTOR:], in_=src[:, W1_VECTOR:])
+            c = codes.tile([P, H], U32, name="w1_c", align_bytes=64)
+            s = codes.tile([P, H], U8, name="w1_s", align_bytes=64)
+            nc.vector.quantize_mx(out=c[:].bitcast(FP8X4), scales=s[:], in_=grouped[:])
+            w1_codes[e] = (c, s)
+
+        def prep_w2(e):
+            grouped = mid.tile([P, N * PACK], BF16, name="w2_grouped", align_bytes=64)
+            c = codes.tile([P, N], U32, name="w2_c", align_bytes=64)
+            s = codes.tile([P, N], U8, name="w2_s", align_bytes=64)
+            interleave(nc.vector.tensor_copy, grouped[:, : W2_VECTOR * PACK], w2_raw[e][:, :, :W2_VECTOR])
+            interleave(nc.scalar.copy, grouped[:, W2_VECTOR * PACK :], w2_raw[e][:, :, W2_VECTOR:])
+            nc.vector.quantize_mx(out=c[:].bitcast(FP8X4), scales=s[:], in_=grouped[:])
+            w2_codes[e] = (c, s)
+
+        h_codes = {}
+
+        def layer1(e):
+            c, s = w1_codes[e]
+            cols = slice(e * C, (e + 1) * C)
+            acc = ps1.tile([P, PACK, C], F32, name="acc1")
+            for t in range(PACK):
+                nc.tensor.matmul_mx(
+                    out=acc[:, t, :],
+                    lhsT=c[:, t * P : (t + 1) * P].bitcast(FP8X4),
+                    lhsT_scale=s[:, t * P : (t + 1) * P],
+                    rhs=tok_c[:, cols].bitcast(FP8X4),
+                    rhs_scale=tok_s[:, cols],
+                    start=True,
+                    stop=True,
+                )
+            h = mid.tile([P, C * PACK], BF16, name="h", align_bytes=64)
+            nc.scalar.activation(
+                h[:].rearrange("p (n t) -> p n t", t=PACK), acc[:].rearrange("p t n -> p n t"), RELU
+            )
+            hc = codes.tile([P, C], U32, name="h_c", align_bytes=64)
+            hs = codes.tile([P, C], U8, name="h_s", align_bytes=64)
+            nc.vector.quantize_mx(out=hc[:].bitcast(FP8X4), scales=hs[:], in_=h[:])
+            h_codes[e] = (hc, hs)
+
+        def layer2(e):
+            c, s = w2_codes[e]
+            hc, hs = h_codes[e]
+            acc = ps2.tile([P, BLOCKS, C], F32, name="acc2")
+            for b in range(BLOCKS):
+                nc.tensor.matmul_mx(
+                    out=acc[:, b, :],
+                    lhsT=c[:, b * P : (b + 1) * P].bitcast(FP8X4),
+                    lhsT_scale=s[:, b * P : (b + 1) * P],
+                    rhs=hc[:].bitcast(FP8X4),
+                    rhs_scale=hs[:],
+                    start=True,
+                    stop=True,
+                )
+            g, first = e // GE, (e % GE) * C
+            nc.scalar.copy(out=sums[g][:, :, first : first + C], in_=acc[:])
+
+        def scatter(g, b):
+            nc.vector.tensor_tensor(
+                windows[b][:].indirect(offsets[:, g * GS // 16 : (g + 1) * GS // 16]),
+                sums[g][:, b, :],
+                gates[g][b][:],
+                MULT,
+            )
+
+        nc.sync.dma_start(offsets[:], offs)
+        for t in range(PACK):
+            load_plane(t)
+        for g in range(GROUPS):
+            for e in range(g * GE, (g + 1) * GE):
+                load_w1(e)
+            for e in range(g * GE, (g + 1) * GE):
+                load_w2(e)
+            for b in range(BLOCKS):
+                load_gate(g, b)
+            if g == 0:
+                for t in range(PACK):
+                    nc.vector.tensor_copy(picked[:, t, :], planes[t][:].indirect(offsets[:]))
+                for gt in range(GROUPS):
+                    cols = slice(gt * GS, (gt + 1) * GS)
+                    flat = tok[:, cols, :].rearrange("p n t -> p (n t)")
+                    interleave(nc.vector.tensor_copy, flat, picked[:, :, cols])
+                    nc.vector.quantize_mx(out=tok_c[:, cols].bitcast(FP8X4), scales=tok_s[:, cols], in_=flat)
+            for e in range(g * GE, (g + 1) * GE):
+                prep_w1(e)
+            for e in range(g * GE, (g + 1) * GE):
+                layer1(e)
+            for e in range(g * GE, (g + 1) * GE):
+                prep_w2(e)
+                layer2(e)
+            for b in range(BLOCKS):
+                scatter(g, b)
+                if g == GROUPS - 1:
+                    nc.sync.dma_start(out[b * P : (b + 1) * P, :], windows[b][:])

@@ -12,7 +12,6 @@ U32 = mybir.dt.uint32
 U16 = mybir.dt.uint16
 U8 = mybir.dt.uint8
 FP8X4 = mybir.dt.float8_e4m3fn_x4
-COPY = mybir.ActivationFunctionType.Copy
 RELU = mybir.ActivationFunctionType.Relu
 MULT = mybir.AluOpType.mult
 
@@ -22,13 +21,12 @@ BLOCKS = N // P
 GROUPS = 2
 GE = E // GROUPS
 GS = SLOTS // GROUPS
-W1_VECTOR = 48
-W2_VECTOR = 128
+PAIR = 2
 
 
 def interleave(copy, out, in_):
     copy(
-        out=out.rearrange("p (c i t) -> p c t i", i=PACK, t=PACK),
+        out=out.rearrange("p (c i) t -> p c t i", i=PACK),
         in_=in_.rearrange("p t (c i) -> p c t i", i=PACK),
     )
 
@@ -39,143 +37,182 @@ def tile_routed_moe_kernel(tc, xT, w1, w2, gate, offs, out):
         keep = ctx.enter_context(tc.tile_pool(name="keep", bufs=1))
         wide = ctx.enter_context(tc.tile_pool(name="wide", bufs=6))
         raw1 = ctx.enter_context(tc.tile_pool(name="raw1", bufs=4))
-        raw2 = ctx.enter_context(tc.tile_pool(name="raw2", bufs=4))
-        mid = ctx.enter_context(tc.tile_pool(name="mid", bufs=3))
+        raw2 = ctx.enter_context(tc.tile_pool(name="raw2", bufs=2))
+        groups = ctx.enter_context(tc.tile_pool(name="groups", bufs=4))
         codes = ctx.enter_context(tc.tile_pool(name="codes", bufs=4))
+        codes2 = ctx.enter_context(tc.tile_pool(name="codes2", bufs=3))
         ps1 = ctx.enter_context(tc.psum_pool(name="ps1", bufs=4))
-        ps2 = ctx.enter_context(tc.psum_pool(name="ps2", bufs=4))
+        ps2 = ctx.enter_context(tc.psum_pool(name="ps2", bufs=3))
 
         offsets = keep.tile([P, SLOTS // 16], U16, name="offsets")
-        planes = {}
         picked = keep.tile([P, PACK, SLOTS], F32, name="picked")
         tok = keep.tile([P, SLOTS, PACK], BF16, name="tok", align_bytes=64)
         tok_c = keep.tile([P, SLOTS], U32, name="tok_c", align_bytes=64)
         tok_s = keep.tile([P, SLOTS], U8, name="tok_s", align_bytes=64)
-        windows = {}
-        gates = [[keep.tile([P, GS], F32, name=f"gate{g}_{b}") for b in range(BLOCKS)] for g in range(GROUPS)]
+        gates = [keep.tile([P, BLOCKS, GS], F32, name=f"gate{g}") for g in range(GROUPS)]
         sums = [keep.tile([P, BLOCKS, GS], F32, name=f"sums{g}") for g in range(GROUPS)]
-
-        for b in range(BLOCKS):
-            windows[b] = wide.tile([P, T], F32, name="wide_tile")
-        nc.vector.memset(windows[0][:], 0.0)
-        nc.gpsimd.memset(windows[1][:], 0.0)
-
-        x_planes = xT.rearrange("(p t) n -> p t n", t=PACK)
-        w1_raw, w2_raw = {}, {}
-
-        def load_plane(t):
-            planes[t] = wide.tile([P, T], F32, name="wide_tile")
-            nc.sync.dma_start(planes[t][:], x_planes[:, t, :])
+        windows = [wide.tile([P, T], F32, name="wide_tile") for b in range(BLOCKS)]
+        planes = [wide.tile([P, T], F32, name="wide_tile") for t in range(PACK)]
+        w1_raw, w2_raw, w1_codes, w2_codes, h_codes = {}, {}, {}, {}, {}
 
         def load_w1(e):
             w1_raw[e] = raw1.tile([P, PACK, H], F32, name="w1_raw")
             nc.sync.dma_start(w1_raw[e][:], w1[e].rearrange("(p j) h -> p j h", j=PACK))
 
-        def load_w2(e):
-            w2_raw[e] = raw2.tile([P, PACK, N], F32, name="w2_raw")
-            nc.sync.dma_start(w2_raw[e][:], w2[e].rearrange("(p j) n -> p j n", j=PACK))
+        def load_w2(pair):
+            w2_raw[pair] = raw2.tile([P, PAIR, PACK, N], F32, name="w2_raw")
+            experts = slice(PAIR * pair, PAIR * (pair + 1))
+            nc.sync.dma_start(w2_raw[pair][:], w2[experts].rearrange("e (p j) n -> p e (j n)", j=PACK))
 
-        def load_gate(g, b):
-            nc.sync.dma_start(gates[g][b][:], gate[b * P : (b + 1) * P, g * GS : (g + 1) * GS])
+        def load_gate(g, blocks):
+            rows = gate.rearrange("(b p) s -> p b s", p=P)
+            nc.sync.dma_start(gates[g][:, blocks, :], rows[:, blocks, g * GS : (g + 1) * GS])
 
-        w1_codes, w2_codes = {}, {}
+        def quantize(codes_out, scales_out, values):
+            nc.vector.quantize_mx(out=codes_out.bitcast(FP8X4), scales=scales_out, in_=values)
 
         def prep_w1(e):
-            grouped = mid.tile([P, H * PACK], BF16, name="w1_grouped", align_bytes=64)
-            dst = grouped[:].rearrange("p (t m j) -> p m j t", t=PACK, j=PACK)
-            src = w1_raw[e][:].rearrange("p j (m t) -> p m j t", t=PACK)
-            nc.vector.tensor_copy(out=dst[:, :W1_VECTOR], in_=src[:, :W1_VECTOR])
-            nc.scalar.copy(out=dst[:, W1_VECTOR:], in_=src[:, W1_VECTOR:])
+            grouped = groups.tile([P, H * PACK], BF16, name="grouped", align_bytes=64)
+            nc.scalar.copy(
+                out=grouped[:].rearrange("p (t m j) -> p m j t", t=PACK, j=PACK),
+                in_=w1_raw[e][:].rearrange("p j (m t) -> p m j t", t=PACK),
+            )
             c = codes.tile([P, H], U32, name="w1_c", align_bytes=64)
             s = codes.tile([P, H], U8, name="w1_s", align_bytes=64)
-            nc.vector.quantize_mx(out=c[:].bitcast(FP8X4), scales=s[:], in_=grouped[:])
+            quantize(c[:], s[:], grouped[:])
             w1_codes[e] = (c, s)
 
-        def prep_w2(e):
-            grouped = mid.tile([P, N * PACK], BF16, name="w2_grouped", align_bytes=64)
-            c = codes.tile([P, N], U32, name="w2_c", align_bytes=64)
-            s = codes.tile([P, N], U8, name="w2_s", align_bytes=64)
-            interleave(nc.vector.tensor_copy, grouped[:, : W2_VECTOR * PACK], w2_raw[e][:, :, :W2_VECTOR])
-            interleave(nc.scalar.copy, grouped[:, W2_VECTOR * PACK :], w2_raw[e][:, :, W2_VECTOR:])
-            nc.vector.quantize_mx(out=c[:].bitcast(FP8X4), scales=s[:], in_=grouped[:])
-            w2_codes[e] = (c, s)
+        def prep_w2(pair, b0, nb):
+            width = nb * P
+            grouped = groups.tile([P, PAIR * N * PACK], BF16, name="grouped", align_bytes=64)
+            values = grouped[:, : PAIR * width * PACK]
+            dst = values.rearrange("p (e n j) -> p e n j", e=PAIR, j=PACK)
+            for k in range(PAIR):
+                interleave(nc.vector.tensor_copy, dst[:, k], w2_raw[pair][:, k, :, b0 * P : b0 * P + width])
+            c = codes2.tile([P, PAIR * N], U32, name=f"w2_c{b0}", align_bytes=64)
+            s = codes2.tile([P, PAIR * N], U8, name=f"w2_s{b0}", align_bytes=64)
+            used = slice(0, PAIR * width)
+            quantize(c[:, used], s[:, used], values)
+            w2_codes[pair] = (c, s)
 
-        h_codes = {}
+        def layer1(pair):
+            grouped = groups.tile([P, PAIR * N * PACK], BF16, name="grouped", align_bytes=64)
+            values = grouped[:, : PAIR * C * PACK]
+            h = values.rearrange("p (e n t) -> p e n t", e=PAIR, t=PACK)
+            for k in range(PAIR):
+                e = PAIR * pair + k
+                c, s = w1_codes[e]
+                cols = slice(e * C, (e + 1) * C)
+                acc = ps1.tile([P, PACK, C], F32, name="acc1")
+                for t in range(PACK):
+                    nc.tensor.matmul_mx(
+                        out=acc[:, t, :],
+                        lhsT=c[:, t * P : (t + 1) * P].bitcast(FP8X4),
+                        lhsT_scale=s[:, t * P : (t + 1) * P],
+                        rhs=tok_c[:, cols].bitcast(FP8X4),
+                        rhs_scale=tok_s[:, cols],
+                        start=True,
+                        stop=True,
+                    )
+                nc.scalar.activation(h[:, k], acc[:].rearrange("p t n -> p n t"), RELU)
+            hc = codes2.tile([P, PAIR * C], U32, name="h_c", align_bytes=64)
+            hs = codes2.tile([P, PAIR * C], U8, name="h_s", align_bytes=64)
+            quantize(hc[:], hs[:], values)
+            h_codes[pair] = (hc, hs)
 
-        def layer1(e):
-            c, s = w1_codes[e]
-            cols = slice(e * C, (e + 1) * C)
-            acc = ps1.tile([P, PACK, C], F32, name="acc1")
-            for t in range(PACK):
-                nc.tensor.matmul_mx(
-                    out=acc[:, t, :],
-                    lhsT=c[:, t * P : (t + 1) * P].bitcast(FP8X4),
-                    lhsT_scale=s[:, t * P : (t + 1) * P],
-                    rhs=tok_c[:, cols].bitcast(FP8X4),
-                    rhs_scale=tok_s[:, cols],
-                    start=True,
-                    stop=True,
-                )
-            h = mid.tile([P, C * PACK], BF16, name="h", align_bytes=64)
-            nc.scalar.activation(
-                h[:].rearrange("p (n t) -> p n t", t=PACK), acc[:].rearrange("p t n -> p n t"), RELU
+        def layer2(pair, b0, nb):
+            c, s = w2_codes[pair]
+            hc, hs = h_codes[pair]
+            acc = ps2.tile([P, BLOCKS, PAIR, C], F32, name="acc2")
+            for b in range(nb):
+                for k in range(PAIR):
+                    feats = slice((k * nb + b) * P, (k * nb + b + 1) * P)
+                    slots = slice(k * C, (k + 1) * C)
+                    nc.tensor.matmul_mx(
+                        out=acc[:, b, k, :],
+                        lhsT=c[:, feats].bitcast(FP8X4),
+                        lhsT_scale=s[:, feats],
+                        rhs=hc[:, slots].bitcast(FP8X4),
+                        rhs_scale=hs[:, slots],
+                        start=True,
+                        stop=True,
+                    )
+            first = (pair * PAIR % GE) * C
+            nc.scalar.copy(
+                out=sums[pair * PAIR // GE][:, b0 : b0 + nb, first : first + PAIR * C],
+                in_=acc[:, :nb].rearrange("p b k n -> p b (k n)"),
             )
-            hc = codes.tile([P, C], U32, name="h_c", align_bytes=64)
-            hs = codes.tile([P, C], U8, name="h_s", align_bytes=64)
-            nc.vector.quantize_mx(out=hc[:].bitcast(FP8X4), scales=hs[:], in_=h[:])
-            h_codes[e] = (hc, hs)
-
-        def layer2(e):
-            c, s = w2_codes[e]
-            hc, hs = h_codes[e]
-            acc = ps2.tile([P, BLOCKS, C], F32, name="acc2")
-            for b in range(BLOCKS):
-                nc.tensor.matmul_mx(
-                    out=acc[:, b, :],
-                    lhsT=c[:, b * P : (b + 1) * P].bitcast(FP8X4),
-                    lhsT_scale=s[:, b * P : (b + 1) * P],
-                    rhs=hc[:].bitcast(FP8X4),
-                    rhs_scale=hs[:],
-                    start=True,
-                    stop=True,
-                )
-            g, first = e // GE, (e % GE) * C
-            nc.scalar.copy(out=sums[g][:, :, first : first + C], in_=acc[:])
 
         def scatter(g, b):
             nc.vector.tensor_tensor(
                 windows[b][:].indirect(offsets[:, g * GS // 16 : (g + 1) * GS // 16]),
                 sums[g][:, b, :],
-                gates[g][b][:],
+                gates[g][:, b, :],
                 MULT,
             )
 
+        def gather(t):
+            nc.vector.tensor_copy(picked[:, t, :], planes[t][:].indirect(offsets[:]))
+
+        def store(b):
+            nc.sync.dma_start(out[b * P : (b + 1) * P, :], windows[b][:])
+
         nc.sync.dma_start(offsets[:], offs)
-        for t in range(PACK):
+        nc.vector.memset(windows[0][:], 0.0)
+        nc.gpsimd.memset(windows[1][:], 0.0)
+        x_planes = xT.rearrange("(p t) n -> p t n", t=PACK)
+        def load_plane(t):
+            nc.sync.dma_start(planes[t][:], x_planes[:, t, :])
+
+        def interleave_planes(first, cols):
+            nc.vector.tensor_copy(
+                out=tok[:, cols, first : first + 2],
+                in_=picked[:, first : first + 2, cols].rearrange("p t n -> p n t"),
+            )
+
+        load_plane(0)
+        load_w1(0)
+        for t in range(1, PACK):
             load_plane(t)
+        prep_w1(0)
+        for e in range(1, GE):
+            load_w1(e)
+        for pair in (0, 1):
+            load_w2(pair)
+        load_gate(0, slice(0, BLOCKS))
+        gather(0)
+        gather(1)
+        interleave_planes(0, slice(0, SLOTS))
+        gather(2)
+        gather(3)
         for g in range(GROUPS):
-            for e in range(g * GE, (g + 1) * GE):
-                load_w1(e)
-            for e in range(g * GE, (g + 1) * GE):
-                load_w2(e)
-            for b in range(BLOCKS):
-                load_gate(g, b)
-            if g == 0:
-                for t in range(PACK):
-                    nc.vector.tensor_copy(picked[:, t, :], planes[t][:].indirect(offsets[:]))
-                for gt in range(GROUPS):
-                    cols = slice(gt * GS, (gt + 1) * GS)
-                    flat = tok[:, cols, :].rearrange("p n t -> p (n t)")
-                    interleave(nc.vector.tensor_copy, flat, picked[:, :, cols])
-                    nc.vector.quantize_mx(out=tok_c[:, cols].bitcast(FP8X4), scales=tok_s[:, cols], in_=flat)
-            for e in range(g * GE, (g + 1) * GE):
-                prep_w1(e)
-            for e in range(g * GE, (g + 1) * GE):
-                layer1(e)
-            for e in range(g * GE, (g + 1) * GE):
-                prep_w2(e)
-                layer2(e)
-            for b in range(BLOCKS):
-                scatter(g, b)
-                if g == GROUPS - 1:
-                    nc.sync.dma_start(out[b * P : (b + 1) * P, :], windows[b][:])
+            cols = slice(g * GS, (g + 1) * GS)
+            interleave_planes(2, cols)
+            quantize(tok_c[:, cols], tok_s[:, cols], tok[:, cols, :].rearrange("p n t -> p (n t)"))
+        for e in range(1, GE):
+            prep_w1(e)
+        layer1(0)
+        prep_w2(0, 0, BLOCKS)
+        layer1(1)
+        layer2(0, 0, BLOCKS)
+        prep_w2(1, 0, BLOCKS)
+        layer2(1, 0, BLOCKS)
+        for e in range(GE, E):
+            load_w1(e)
+        for pair in (2, 3):
+            load_w2(pair)
+        for b in range(BLOCKS):
+            load_gate(1, slice(b, b + 1))
+        scatter(0, 0)
+        scatter(0, 1)
+        for e in range(GE, E):
+            prep_w1(e)
+        layer1(2)
+        prep_w2(2, 0, BLOCKS)
+        layer1(3)
+        layer2(2, 0, BLOCKS)
+        for b in range(BLOCKS):
+            prep_w2(3, b, 1)
+            layer2(3, b, 1)
+            scatter(1, b)
+            store(b)

@@ -60,9 +60,9 @@ def tile_routed_moe_kernel(tc, xT, w1, w2, gate, offs, out):
             nc.sync.dma_start(w1_raw[e][:], w1[e].rearrange("(p j) h -> p j h", j=PACK))
 
         def load_w2(pair):
-            w2_raw[pair] = raw2.tile([P, PAIR, PACK, N], F32, name="w2_raw")
-            experts = slice(PAIR * pair, PAIR * (pair + 1))
-            nc.sync.dma_start(w2_raw[pair][:], w2[experts].rearrange("e (p j) n -> p e (j n)", j=PACK))
+            w2_raw[pair] = raw2.tile([P, PACK, PAIR, N], F32, name="w2_raw")
+            for k in range(PAIR):
+                nc.sync.dma_start(w2_raw[pair][:, :, k, :], w2[PAIR * pair + k].rearrange("(p j) n -> p j n", j=PACK))
 
         def load_gate(g, blocks):
             rows = gate.rearrange("(b p) s -> p b s", p=P)
@@ -86,9 +86,13 @@ def tile_routed_moe_kernel(tc, xT, w1, w2, gate, offs, out):
             width = nb * P
             grouped = groups.tile([P, PAIR * N * PACK], BF16, name="grouped", align_bytes=64)
             values = grouped[:, : PAIR * width * PACK]
-            dst = values.rearrange("p (e n j) -> p e n j", e=PAIR, j=PACK)
-            for k in range(PAIR):
-                interleave(nc.vector.tensor_copy, dst[:, k], w2_raw[pair][:, k, :, b0 * P : b0 * P + width])
+            raw = w2_raw[pair][:, :, :, b0 * P : b0 * P + width]
+            if nb == BLOCKS:
+                interleave(nc.vector.tensor_copy, values.rearrange("p (n j) -> p n j", j=PACK), raw.rearrange("p j e n -> p j (e n)"))
+            else:
+                dst = values.rearrange("p (e n j) -> p e n j", e=PAIR, j=PACK)
+                for k in range(PAIR):
+                    interleave(nc.vector.tensor_copy, dst[:, k], raw[:, :, k])
             c = codes2.tile([P, PAIR * N], U32, name=f"w2_c{b0}", align_bytes=64)
             s = codes2.tile([P, PAIR * N], U8, name=f"w2_s{b0}", align_bytes=64)
             used = slice(0, PAIR * width)
@@ -164,32 +168,29 @@ def tile_routed_moe_kernel(tc, xT, w1, w2, gate, offs, out):
         def load_plane(t):
             nc.sync.dma_start(planes[t][:], x_planes[:, t, :])
 
-        def interleave_planes(first, cols):
-            nc.vector.tensor_copy(
+        def interleave_planes(copy, first, cols):
+            copy(
                 out=tok[:, cols, first : first + 2],
                 in_=picked[:, first : first + 2, cols].rearrange("p t n -> p n t"),
             )
 
-        load_plane(0)
-        load_w1(0)
-        for t in range(1, PACK):
+        for t in range(PACK):
             load_plane(t)
-        prep_w1(0)
-        for e in range(1, GE):
+        for e in range(0, GE):
             load_w1(e)
         for pair in (0, 1):
             load_w2(pair)
-        load_gate(0, slice(0, BLOCKS))
+        load_gate(0, slice(0, 1))
         gather(0)
         gather(1)
-        interleave_planes(0, slice(0, SLOTS))
+        interleave_planes(nc.vector.tensor_copy, 0, slice(0, SLOTS))
         gather(2)
         gather(3)
         for g in range(GROUPS):
             cols = slice(g * GS, (g + 1) * GS)
-            interleave_planes(2, cols)
+            interleave_planes(nc.vector.tensor_copy, 2, cols)
             quantize(tok_c[:, cols], tok_s[:, cols], tok[:, cols, :].rearrange("p n t -> p (n t)"))
-        for e in range(1, GE):
+        for e in range(0, GE):
             prep_w1(e)
         layer1(0)
         prep_w2(0, 0, BLOCKS)
@@ -197,16 +198,21 @@ def tile_routed_moe_kernel(tc, xT, w1, w2, gate, offs, out):
         layer2(0, 0, BLOCKS)
         prep_w2(1, 0, BLOCKS)
         layer2(1, 0, BLOCKS)
-        for e in range(GE, E):
-            load_w1(e)
+        load_w1(4)
+        load_w1(5)
+        load_gate(0, slice(1, 2))
+        load_w1(6)
+        load_w1(7)
         for pair in (2, 3):
             load_w2(pair)
         for b in range(BLOCKS):
             load_gate(1, slice(b, b + 1))
         scatter(0, 0)
+        prep_w1(4)
+        prep_w1(5)
         scatter(0, 1)
-        for e in range(GE, E):
-            prep_w1(e)
+        prep_w1(6)
+        prep_w1(7)
         layer1(2)
         prep_w2(2, 0, BLOCKS)
         layer1(3)

@@ -22,6 +22,8 @@ GROUPS = 2
 GE = E // GROUPS
 GS = SLOTS // GROUPS
 PAIR = 2
+W1_VECTOR = (0, 64, 64, 64, 0, 0, 0, 0)
+W2_VECTOR = (512, 512, 512, 512)
 
 
 def interleave(copy, out, in_):
@@ -73,10 +75,12 @@ def tile_routed_moe_kernel(tc, xT, w1, w2, gate, offs, out):
 
         def prep_w1(e):
             grouped = groups.tile([P, H * PACK], BF16, name="grouped", align_bytes=64)
-            nc.scalar.copy(
-                out=grouped[:].rearrange("p (t m j) -> p m j t", t=PACK, j=PACK),
-                in_=w1_raw[e][:].rearrange("p j (m t) -> p m j t", t=PACK),
-            )
+            dst = grouped[:].rearrange("p (t m j) -> p m j t", t=PACK, j=PACK)
+            src = w1_raw[e][:].rearrange("p j (m t) -> p m j t", t=PACK)
+            cut = W1_VECTOR[e]
+            if cut > 0:
+                nc.vector.tensor_copy(out=dst[:, :cut], in_=src[:, :cut])
+            nc.scalar.copy(out=dst[:, cut:], in_=src[:, cut:])
             c = codes.tile([P, H], U32, name="w1_c", align_bytes=64)
             s = codes.tile([P, H], U8, name="w1_s", align_bytes=64)
             quantize(c[:], s[:], grouped[:])
@@ -88,7 +92,12 @@ def tile_routed_moe_kernel(tc, xT, w1, w2, gate, offs, out):
             values = grouped[:, : PAIR * width * PACK]
             raw = w2_raw[pair][:, :, :, b0 * P : b0 * P + width]
             if nb == BLOCKS:
-                interleave(nc.vector.tensor_copy, values.rearrange("p (n j) -> p n j", j=PACK), raw.rearrange("p j e n -> p j (e n)"))
+                dst = values.rearrange("p (n j) -> p n j", j=PACK)
+                src = raw.rearrange("p j e n -> p j (e n)")
+                cut = W2_VECTOR[pair]
+                interleave(nc.vector.tensor_copy, dst[:, :cut], src[:, :, :cut])
+                if cut < PAIR * N:
+                    interleave(nc.scalar.copy, dst[:, cut:], src[:, :, cut:])
             else:
                 dst = values.rearrange("p (e n j) -> p e n j", e=PAIR, j=PACK)
                 for k in range(PAIR):

@@ -23,7 +23,7 @@ GE = E // GROUPS
 GS = SLOTS // GROUPS
 PAIR = 2
 W1_VECTOR = (0, 64, 64, 64, 0, 0, 0, 0)
-W2_VECTOR = (512, 512, 512, 512)
+W2_VECTOR = (512, 256, 256, 512)
 
 
 def interleave(copy, out, in_):
@@ -195,10 +195,8 @@ def tile_routed_moe_kernel(tc, xT, w1, w2, gate, offs, out):
         interleave_planes(nc.vector.tensor_copy, 0, slice(0, SLOTS))
         gather(2)
         gather(3)
-        for g in range(GROUPS):
-            cols = slice(g * GS, (g + 1) * GS)
-            interleave_planes(nc.vector.tensor_copy, 2, cols)
-            quantize(tok_c[:, cols], tok_s[:, cols], tok[:, cols, :].rearrange("p n t -> p (n t)"))
+        interleave_planes(nc.vector.tensor_copy, 2, slice(0, SLOTS))
+        quantize(tok_c[:], tok_s[:], tok[:].rearrange("p n t -> p (n t)"))
         for e in range(0, GE):
             prep_w1(e)
         layer1(0)

from contextlib import ExitStack

import concourse.mybir as mybir

K, T, E, C, H, N = 512, 4096, 8, 128, 512, 256
SLOTS = E * C
FLOPS = 2 * SLOTS * (K * H + H * N)

F32 = mybir.dt.float32
BF16 = mybir.dt.bfloat16
U32 = mybir.dt.uint32
U16 = mybir.dt.uint16
U8 = mybir.dt.uint8
FP8X4 = mybir.dt.float8_e4m3fn_x4
RELU = mybir.ActivationFunctionType.Relu
MULT = mybir.AluOpType.mult

P = 128
PACK = 4
BLOCKS = N // P
GROUPS = 2
GE = E // GROUPS
GS = SLOTS // GROUPS
PAIR = 2
W1_VECTOR = (0, 64, 64, 64, 0, 0, 0, 0)
W2_VECTOR = (512, 256, 256, 512)


def interleave(copy, out, in_):
    copy(
        out=out.rearrange("p (c i) t -> p c t i", i=PACK),
        in_=in_.rearrange("p t (c i) -> p c t i", i=PACK),
    )


def tile_routed_moe_kernel(tc, xT, w1, w2, gate, offs, out):
    nc = tc.nc
    with ExitStack() as ctx:
        keep = ctx.enter_context(tc.tile_pool(name="keep", bufs=1))
        wide = ctx.enter_context(tc.tile_pool(name="wide", bufs=6))
        raw1 = ctx.enter_context(tc.tile_pool(name="raw1", bufs=4))
        raw2 = ctx.enter_context(tc.tile_pool(name="raw2", bufs=2))
        groups = ctx.enter_context(tc.tile_pool(name="groups", bufs=4))
        codes = ctx.enter_context(tc.tile_pool(name="codes", bufs=4))
        codes2 = ctx.enter_context(tc.tile_pool(name="codes2", bufs=3))
        ps1 = ctx.enter_context(tc.psum_pool(name="ps1", bufs=4))
        ps2 = ctx.enter_context(tc.psum_pool(name="ps2", bufs=3))

        offsets = keep.tile([P, SLOTS // 16], U16, name="offsets")
        picked = keep.tile([P, PACK, SLOTS], F32, name="picked")
        tok = keep.tile([P, SLOTS, PACK], BF16, name="tok", align_bytes=64)
        tok_c = keep.tile([P, SLOTS], U32, name="tok_c", align_bytes=64)
        tok_s = keep.tile([P, SLOTS], U8, name="tok_s", align_bytes=64)
        gates = [keep.tile([P, BLOCKS, GS], F32, name=f"gate{g}") for g in range(GROUPS)]
        sums = [keep.tile([P, BLOCKS, GS], F32, name=f"sums{g}") for g in range(GROUPS)]
        windows = [wide.tile([P, T], F32, name="wide_tile") for b in range(BLOCKS)]
        planes = [wide.tile([P, T], F32, name="wide_tile") for t in range(PACK)]
        w1_raw, w2_raw, w1_codes, w2_codes, h_codes = {}, {}, {}, {}, {}

        def load_w1(e):
            w1_raw[e] = raw1.tile([P, PACK, H], F32, name="w1_raw")
            nc.sync.dma_start(w1_raw[e][:], w1[e].rearrange("(p j) h -> p j h", j=PACK))

        def load_w2(pair):
            w2_raw[pair] = raw2.tile([P, PACK, PAIR, N], F32, name="w2_raw")
            for k in range(PAIR):
                nc.sync.dma_start(w2_raw[pair][:, :, k, :], w2[PAIR * pair + k].rearrange("(p j) n -> p j n", j=PACK))

        def load_gate(g, blocks):
            rows = gate.rearrange("(b p) s -> p b s", p=P)
            nc.sync.dma_start(gates[g][:, blocks, :], rows[:, blocks, g * GS : (g + 1) * GS])

        def quantize(codes_out, scales_out, values):
            nc.vector.quantize_mx(out=codes_out.bitcast(FP8X4), scales=scales_out, in_=values)

        def prep_w1(e):
            grouped = groups.tile([P, H * PACK], BF16, name="grouped", align_bytes=64)
            dst = grouped[:].rearrange("p (t m j) -> p m j t", t=PACK, j=PACK)
            src = w1_raw[e][:].rearrange("p j (m t) -> p m j t", t=PACK)
            cut = W1_VECTOR[e]
            if cut > 0:
                nc.vector.tensor_copy(out=dst[:, :cut], in_=src[:, :cut])
            nc.scalar.copy(out=dst[:, cut:], in_=src[:, cut:])
            c = codes.tile([P, H], U32, name="w1_c", align_bytes=64)
            s = codes.tile([P, H], U8, name="w1_s", align_bytes=64)
            quantize(c[:], s[:], grouped[:])
            w1_codes[e] = (c, s)

        def prep_w2(pair, b0, nb):
            width = nb * P
            grouped = groups.tile([P, PAIR * N * PACK], BF16, name="grouped", align_bytes=64)
            values = grouped[:, : PAIR * width * PACK]
            raw = w2_raw[pair][:, :, :, b0 * P : b0 * P + width]
            if nb == BLOCKS:
                dst = values.rearrange("p (n j) -> p n j", j=PACK)
                src = raw.rearrange("p j e n -> p j (e n)")
                cut = W2_VECTOR[pair]
                interleave(nc.vector.tensor_copy, dst[:, :cut], src[:, :, :cut])
                if cut < PAIR * N:
                    interleave(nc.scalar.copy, dst[:, cut:], src[:, :, cut:])
            else:
                dst = values.rearrange("p (e n j) -> p e n j", e=PAIR, j=PACK)
                for k in range(PAIR):
                    interleave(nc.vector.tensor_copy, dst[:, k], raw[:, :, k])
            c = codes2.tile([P, PAIR * N], U32, name=f"w2_c{b0}", align_bytes=64)
            s = codes2.tile([P, PAIR * N], U8, name=f"w2_s{b0}", align_bytes=64)
            used = slice(0, PAIR * width)
            quantize(c[:, used], s[:, used], values)
            w2_codes[pair] = (c, s)

        def layer1(pair):
            grouped = groups.tile([P, PAIR * N * PACK], BF16, name="grouped", align_bytes=64)
            values = grouped[:, : PAIR * C * PACK]
            h = values.rearrange("p (e n t) -> p e n t", e=PAIR, t=PACK)
            for k in range(PAIR):
                e = PAIR * pair + k
                c, s = w1_codes[e]
                cols = slice(e * C, (e + 1) * C)
                acc = ps1.tile([P, PACK, C], F32, name="acc1")
                for t in range(PACK):
                    nc.tensor.matmul_mx(
                        out=acc[:, t, :],
                        lhsT=c[:, t * P : (t + 1) * P].bitcast(FP8X4),
                        lhsT_scale=s[:, t * P : (t + 1) * P],
                        rhs=tok_c[:, cols].bitcast(FP8X4),
                        rhs_scale=tok_s[:, cols],
                        start=True,
                        stop=True,
                    )
                nc.scalar.activation(h[:, k], acc[:].rearrange("p t n -> p n t"), RELU)
            hc = codes2.tile([P, PAIR * C], U32, name="h_c", align_bytes=64)
            hs = codes2.tile([P, PAIR * C], U8, name="h_s", align_bytes=64)
            quantize(hc[:], hs[:], values)
            h_codes[pair] = (hc, hs)

        def layer2(pair, b0, nb):
            c, s = w2_codes[pair]
            hc, hs = h_codes[pair]
            acc = ps2.tile([P, BLOCKS, PAIR, C], F32, name="acc2")
            for b in range(nb):
                for k in range(PAIR):
                    feats = slice((k * nb + b) * P, (k * nb + b + 1) * P)
                    slots = slice(k * C, (k + 1) * C)
                    nc.tensor.matmul_mx(
                        out=acc[:, b, k, :],
                        lhsT=c[:, feats].bitcast(FP8X4),
                        lhsT_scale=s[:, feats],
                        rhs=hc[:, slots].bitcast(FP8X4),
                        rhs_scale=hs[:, slots],
                        start=True,
                        stop=True,
                    )
            first = (pair * PAIR % GE) * C
            nc.scalar.copy(
                out=sums[pair * PAIR // GE][:, b0 : b0 + nb, first : first + PAIR * C],
                in_=acc[:, :nb].rearrange("p b k n -> p b (k n)"),
            )

        def scatter(g, b):
            nc.vector.tensor_tensor(
                windows[b][:].indirect(offsets[:, g * GS // 16 : (g + 1) * GS // 16]),
                sums[g][:, b, :],
                gates[g][:, b, :],
                MULT,
            )

        def gather(t):
            nc.vector.tensor_copy(picked[:, t, :], planes[t][:].indirect(offsets[:]))

        def store(b):
            nc.sync.dma_start(out[b * P : (b + 1) * P, :], windows[b][:])

        nc.sync.dma_start(offsets[:], offs)
        nc.vector.memset(windows[0][:], 0.0)
        nc.gpsimd.memset(windows[1][:], 0.0)
        x_planes = xT.rearrange("(p t) n -> p t n", t=PACK)
        def load_plane(t):
            nc.sync.dma_start(planes[t][:], x_planes[:, t, :])

        def interleave_planes(copy, first, cols):
            copy(
                out=tok[:, cols, first : first + 2],
                in_=picked[:, first : first + 2, cols].rearrange("p t n -> p n t"),
            )

        for t in range(PACK):
            load_plane(t)
        for e in range(0, GE):
            load_w1(e)
        for pair in (0, 1):
            load_w2(pair)
        load_gate(0, slice(0, 1))
        gather(0)
        gather(1)
        interleave_planes(nc.vector.tensor_copy, 0, slice(0, SLOTS))
        gather(2)
        gather(3)
        interleave_planes(nc.vector.tensor_copy, 2, slice(0, SLOTS))
        quantize(tok_c[:], tok_s[:], tok[:].rearrange("p n t -> p (n t)"))
        for e in range(0, GE):
            prep_w1(e)
        layer1(0)
        prep_w2(0, 0, BLOCKS)
        layer1(1)
        layer2(0, 0, BLOCKS)
        prep_w2(1, 0, BLOCKS)
        layer2(1, 0, BLOCKS)
        load_w1(4)
        load_w1(5)
        load_gate(0, slice(1, 2))
        load_w1(6)
        load_w1(7)
        for pair in (2, 3):
            load_w2(pair)
        for b in range(BLOCKS):
            load_gate(1, slice(b, b + 1))
        scatter(0, 0)
        prep_w1(4)
        prep_w1(5)
        scatter(0, 1)
        prep_w1(6)
        prep_w1(7)
        layer1(2)
        prep_w2(2, 0, BLOCKS)
        layer1(3)
        layer2(2, 0, BLOCKS)
        for b in range(BLOCKS):
            prep_w2(3, b, 1)
            layer2(3, b, 1)
            scatter(1, b)
            store(b)
